import numpy as np
import ml_dtypes


def mxq(x, axis, fmt="e4m3"):
    dtype, down = {"e4m3": (ml_dtypes.float8_e4m3fn, 7), "e5m2": (ml_dtypes.float8_e5m2, 14)}[fmt]
    v = np.moveaxis(np.asarray(x, np.float32).astype(ml_dtypes.bfloat16).astype(np.float64), axis, -1)
    blocks = v.reshape(v.shape[:-1] + (-1, 32))
    amax = np.abs(blocks).max(-1, keepdims=True)
    byte = np.maximum(np.where(amax > 0, np.frexp(amax)[1] - 1 + 127, 0) - down, 1)
    scale = np.exp2(byte - 127.0)
    codes = (blocks / scale).astype(np.float32).astype(dtype).astype(np.float64)
    return np.moveaxis((codes * scale).reshape(v.shape), -1, axis)


WIDE = False


def mx_kscale(k):
    if not WIDE:
        return np.ones(k)
    levels = np.array([10, -10, 5, -5, 0])
    if k % 512:
        return np.exp2(np.random.permutation(np.resize(levels, k // 32))).repeat(32)
    a = np.empty((k // 512, 16))
    for p in range(k // 512):
        a[p, :8] = np.random.permutation(np.resize(levels, 8))
        for g in range(8):
            far = levels[np.abs(levels - a[p, g]) >= 10]
            a[p, g + 8] = far[np.random.randint(len(far))]
    return np.exp2(a.ravel()).repeat(32)


def f64(x):
    return np.asarray(x).astype(np.float64)


def striped(idx):
    return np.tile(idx.reshape(-1, 16).T, (8, 1)).astype(np.uint16)


def unstriped(offs):
    return offs[:16].T.reshape(-1).astype(np.int64)


def pack_weight(w):
    k, n = w.shape
    w = f64(np.asarray(w, np.float32).astype(ml_dtypes.bfloat16)).reshape(k // 32, 32, n)
    amax = np.abs(w).max(1)
    byte = np.clip(np.where(amax > 0, np.frexp(amax)[1] - 1 + 127 - 7, 1), 1, 254)
    scaled = (w * np.exp2(127.0 - byte)[:, None, :]).reshape(k, n).astype(np.float32)
    words = np.ascontiguousarray(scaled.reshape(k // 512, 128, 4, n).transpose(0, 1, 3, 2)).astype(ml_dtypes.float8_e4m3fn).view(np.uint8)
    return words, np.ascontiguousarray(byte.astype(np.uint8).reshape(k // 512, 16, n))


def unpack_weight(words, scales):
    g, p, n, _ = words.shape
    vals = np.ascontiguousarray(words).view(ml_dtypes.float8_e4m3fn).astype(np.float64) * np.repeat(np.exp2(scales.astype(np.float64) - 127.0), 8, axis=1)[..., None]
    return vals.transpose(0, 1, 3, 2).reshape(g * 512, n)


K, T, S, J, G = 512, 2048, 512, 512, 128


def setup_inputs():
    n = np.random.standard_normal
    s = mx_kscale(K)[:, None]
    packed_xT = pack_weight(n((K, T)) * s)
    packed_eT = pack_weight(n((K, T)) * s)
    packed_fT = pack_weight(n((K, T)) * s)
    return {
        "x_words": packed_xT[0],
        "x_scales": packed_xT[1],
        "e_words": packed_eT[0],
        "e_scales": packed_eT[1],
        "f_words": packed_fT[0],
        "f_scales": packed_fT[1],
        "hT": (n((K, J)) / np.sqrt(3 * K) / s).astype(np.float32),
        "gT": (n((K, J)) / np.sqrt(3 * K) / s).astype(np.float32),
        "rT": (n((K, J)) / np.sqrt(3 * K) / s).astype(np.float32),
        "offs": striped(np.random.permutation(T)[:S]),
        "code2": striped(np.random.permutation(T)[:S]),
        "code3": striped(np.random.permutation(T)[:S]),
    }


def reference(x_words, x_scales, e_words, e_scales, f_words, f_scales, hT, gT, rT, offs, code2, code3):
    hTq = mxq(f64(hT), 0, "e4m3")
    xq = unpack_weight(x_words, x_scales)[:, unstriped(offs)]
    gTq = mxq(f64(gT), 0, "e4m3")
    e_code2 = unpack_weight(e_words, e_scales)[:, unstriped(code2)]
    rTq = mxq(f64(rT), 0, "e4m3")
    f_code3 = unpack_weight(f_words, f_scales)[:, unstriped(code3)]
    y = hTq.T @ xq + gTq.T @ e_code2 + rTq.T @ f_code3
    return y.reshape(J, G, 4).max(axis=2)

@@ -1,0 +1,126 @@
+from contextlib import ExitStack
+
+import concourse.mybir as mybir
+
+K, T, S, J, G = 512, 2048, 512, 512, 128
+FLOPS = 2 * 3 * K * J * S
+
+F32 = mybir.dt.float32
+BF16 = mybir.dt.bfloat16
+I32 = mybir.dt.int32
+U32 = mybir.dt.uint32
+U16 = mybir.dt.uint16
+U8 = mybir.dt.uint8
+FP8X4 = mybir.dt.float8_e4m3fn_x4
+
+P = 128
+PACK = 4
+BLOCKS = J // P
+
+
+def tile_picked_zpq_max_p_kernel(tc, x_words, x_scales, e_words, e_scales, f_words, f_scales, hT, gT, rT, offs, code2, code3, out):
+    nc = tc.nc
+    with ExitStack() as ctx:
+        keep = ctx.enter_context(tc.tile_pool(name="keep", bufs=1))
+        psum = ctx.enter_context(tc.psum_pool(name="psum", bufs=1))
+
+        def load_list(name, src):
+            tile = keep.tile([P, S // 16], U16, name=name)
+            nc.sync.dma_start(tile[:], src)
+            return tile
+
+        def load_words(name, src):
+            tile = keep.tile([P, T], U32, name=name, align_bytes=64)
+            nc.sync.dma_start(tile[:].bitcast(I32), src[0].rearrange("p n t -> p (n t)").bitcast(I32))
+            return tile
+
+        def cleared_scales(name):
+            tile = keep.tile([P, T], U8, name=name, align_bytes=64)
+            nc.vector.memset(tile[:].bitcast(I32), 0)
+            return tile
+
+        def load_scales(tile, src, first):
+            for q in range(4):
+                row = 32 * q + first
+                nc.sync.dma_start(tile[row : row + 4, :].bitcast(I32), src[0, 4 * q : 4 * q + 4, :].bitcast(I32))
+
+        def load_queries(name, src, c0, width):
+            tile = keep.tile([P, PACK, width], F32, name=name)
+            nc.sync.dma_start(tile[:], src.rearrange("(p j) t -> p j t", j=PACK)[:, :, c0 : c0 + width])
+            return tile
+
+        def gather(name, dtype, window, offsets):
+            tile = keep.tile([P, S], dtype, name=name, align_bytes=64)
+            nc.vector.tensor_copy(tile[:], window[:].indirect(offsets[:]))
+            return tile
+
+        def interleave(name, raw, width):
+            tile = keep.tile([P, width, PACK], BF16, name=name, align_bytes=64)
+            nc.scalar.copy(
+                out=tile[:].rearrange("p (c i) j -> p c j i", i=4),
+                in_=raw[:].rearrange("p j (c i) -> p c j i", i=4),
+            )
+            return tile
+
+        def quantize(name, grouped, width):
+            codes = keep.tile([P, width], U32, name=name + "_codes", align_bytes=64)
+            scales = keep.tile([P, width], U8, name=name + "_scales", align_bytes=64)
+            nc.vector.quantize_mx(out=codes[:].bitcast(FP8X4), scales=scales[:], in_=grouped[:].rearrange("p w j -> p (w j)"))
+            return codes, scales
+
+        x_bytes = cleared_scales("x_bytes")
+        e_bytes = cleared_scales("e_bytes")
+        f_bytes = cleared_scales("f_bytes")
+
+        h_raw = load_queries("h_raw", hT, 0, J)
+        x_list = load_list("x_list", offs)
+        load_scales(x_bytes, x_scales, 0)
+        e_list = load_list("e_list", code2)
+        x_table = load_words("x_table", x_words)
+        load_scales(e_bytes, e_scales, 4)
+        g_raw = load_queries("g_raw", gT, 0, J)
+        f_list = load_list("f_list", code3)
+        load_scales(f_bytes, f_scales, 8)
+        e_table = load_words("e_table", e_words)
+        f_table = load_words("f_table", f_words)
+        r_raw = [load_queries("r_raw%d" % b, rT, b * P, P) for b in range(BLOCKS)]
+
+        acc = [psum.tile([P, S], F32, name="acc%d" % b) for b in range(BLOCKS)]
+
+        def multiply(b, codes, scales, cols, picked, picked_scales, first, start, stop):
+            nc.tensor.matmul_mx(
+                out=acc[b][:],
+                lhsT=codes[:, cols].bitcast(FP8X4),
+                lhsT_scale=scales[:, cols],
+                rhs=picked[:].bitcast(FP8X4),
+                rhs_scale=picked_scales[first:P, :],
+                start=start,
+                stop=stop,
+            )
+
+        x_picked_scales = gather("x_picked_scales", U8, x_bytes, x_list)
+        h_grouped = interleave("h_grouped", h_raw, J)
+        x_picked = gather("x_picked", U32, x_table, x_list)
+        h_codes, h_scales = quantize("h", h_grouped, J)
+        e_picked_scales = gather("e_picked_scales", U8, e_bytes, e_list)
+        for b in range(BLOCKS):
+            multiply(b, h_codes, h_scales, slice(b * P, (b + 1) * P), x_picked, x_picked_scales, 0, True, False)
+        g_grouped = interleave("g_grouped", g_raw, J)
+        f_picked_scales = gather("f_picked_scales", U8, f_bytes, f_list)
+        e_picked = gather("e_picked", U32, e_table, e_list)
+        g_codes, g_scales = quantize("g", g_grouped, J)
+        for b in range(BLOCKS):
+            multiply(b, g_codes, g_scales, slice(b * P, (b + 1) * P), e_picked, e_picked_scales, 4, False, False)
+        f_picked = gather("f_picked", U32, f_table, f_list)
+        for b in range(BLOCKS):
+            r_grouped = interleave("r_grouped%d" % b, r_raw[b], P)
+            r_codes, r_scales = quantize("r%d" % b, r_grouped, P)
+            multiply(b, r_codes, r_scales, slice(0, P), f_picked, f_picked_scales, 8, False, True)
+            best = keep.tile([P, G], F32, name="best%d" % b)
+            nc.vector.tensor_reduce(
+                out=best[:],
+                in_=acc[b][:].rearrange("p (v m) -> p v m", m=4),
+                axis=mybir.AxisListType.X,
+                op=mybir.AluOpType.max,
+            )
+            nc.sync.dma_start(out[b * P : (b + 1) * P, :], best[:])

@@ -16,12 +16,16 @@ FP8X4 = mybir.dt.float8_e4m3fn_x4
 P = 128
 PACK = 4
 BLOCKS = J // P
+SCALE_ROWS = K // 32
+FIRST_ROW = P - SCALE_ROWS
+HALF = J // 2
 
 
 def tile_picked_zpq_max_p_kernel(tc, x_words, x_scales, e_words, e_scales, f_words, f_scales, hT, gT, rT, offs, code2, code3, out):
     nc = tc.nc
     with ExitStack() as ctx:
         keep = ctx.enter_context(tc.tile_pool(name="keep", bufs=1))
+        stage = ctx.enter_context(tc.tile_pool(name="stage", bufs=1))
         psum = ctx.enter_context(tc.psum_pool(name="psum", bufs=1))
 
         def load_list(name, src):
@@ -29,36 +33,28 @@ def tile_picked_zpq_max_p_kernel(tc, x_words, x_scales, e_words, e_scales, f_wor
             nc.sync.dma_start(tile[:], src)
             return tile
 
-        def load_words(name, src):
-            tile = keep.tile([P, T], U32, name=name, align_bytes=64)
+        def load_words(pool, name, src):
+            tile = pool.tile([P, T], U32, name=name, align_bytes=64)
             nc.sync.dma_start(tile[:].bitcast(I32), src[0].rearrange("p n t -> p (n t)").bitcast(I32))
             return tile
 
-        def cleared_scales(name):
+        def load_scales(name, src, engine):
             tile = keep.tile([P, T], U8, name=name, align_bytes=64)
-            nc.vector.memset(tile[:].bitcast(I32), 0)
+            engine.memset(tile[0:FIRST_ROW, :].bitcast(I32), 0)
+            nc.scalar.dma_start(tile[FIRST_ROW:P, :].bitcast(I32), src[0].bitcast(I32))
             return tile
 
-        def load_scales(tile, src, first):
-            for q in range(4):
-                row = 32 * q + first
-                nc.sync.dma_start(tile[row : row + 4, :].bitcast(I32), src[0, 4 * q : 4 * q + 4, :].bitcast(I32))
+        def load_queries(raw, src, first, width):
+            nc.sync.dma_start(raw, src.rearrange("(p j) t -> p j t", j=PACK)[:, :, first : first + width])
 
-        def load_queries(name, src, c0, width):
-            tile = keep.tile([P, PACK, width], F32, name=name)
-            nc.sync.dma_start(tile[:], src.rearrange("(p j) t -> p j t", j=PACK)[:, :, c0 : c0 + width])
-            return tile
-
-        def gather(name, dtype, window, offsets):
-            tile = keep.tile([P, S], dtype, name=name, align_bytes=64)
-            nc.vector.tensor_copy(tile[:], window[:].indirect(offsets[:]))
-            return tile
+        def gather(picked, window, offsets):
+            nc.vector.tensor_copy(picked, window[:].indirect(offsets[:]))
 
         def interleave(name, raw, width):
             tile = keep.tile([P, width, PACK], BF16, name=name, align_bytes=64)
             nc.scalar.copy(
                 out=tile[:].rearrange("p (c i) j -> p c j i", i=4),
-                in_=raw[:].rearrange("p j (c i) -> p c j i", i=4),
+                in_=raw.rearrange("p j (c i) -> p c j i", i=4),
             )
             return tile
 
@@ -68,54 +64,71 @@ def tile_picked_zpq_max_p_kernel(tc, x_words, x_scales, e_words, e_scales, f_wor
             nc.vector.quantize_mx(out=codes[:].bitcast(FP8X4), scales=scales[:], in_=grouped[:].rearrange("p w j -> p (w j)"))
             return codes, scales
 
-        x_bytes = cleared_scales("x_bytes")
-        e_bytes = cleared_scales("e_bytes")
-        f_bytes = cleared_scales("f_bytes")
-
-        h_raw = load_queries("h_raw", hT, 0, J)
         x_list = load_list("x_list", offs)
-        load_scales(x_bytes, x_scales, 0)
+        x_bytes = load_scales("x_bytes", x_scales, nc.vector)
+        h_raw = stage.tile([P, PACK, J], F32, name="first", align_bytes=64)
+        load_queries(h_raw[:], hT, 0, J)
+        e_bytes = load_scales("e_bytes", e_scales, nc.gpsimd)
         e_list = load_list("e_list", code2)
-        x_table = load_words("x_table", x_words)
-        load_scales(e_bytes, e_scales, 4)
-        g_raw = load_queries("g_raw", gT, 0, J)
+        f_bytes = load_scales("f_bytes", f_scales, nc.vector)
         f_list = load_list("f_list", code3)
-        load_scales(f_bytes, f_scales, 8)
-        e_table = load_words("e_table", e_words)
-        f_table = load_words("f_table", f_words)
-        r_raw = [load_queries("r_raw%d" % b, rT, b * P, P) for b in range(BLOCKS)]
+        x_table = load_words(keep, "x_table", x_words)
+        g_raw = stage.tile([P, PACK, HALF], F32, name="second", align_bytes=64)
+        load_queries(g_raw[:], gT, 0, HALF)
+        e_table = load_words(keep, "e_table", e_words)
 
+        picked_bytes = keep.tile([P, 3 * S], U8, name="picked_bytes", align_bytes=64)
+        planes = keep.tile([P, 3 * S], U8, name="planes", align_bytes=64)
+        nc.gpsimd.memset(planes[:].bitcast(I32), 0)
+        x_picked = keep.tile([P, S], U32, name="x_picked", align_bytes=64)
+        e_picked = keep.tile([P, S], U32, name="e_picked", align_bytes=64)
+        f_picked = keep.tile([P, S], U32, name="f_picked", align_bytes=64)
         acc = [psum.tile([P, S], F32, name="acc%d" % b) for b in range(BLOCKS)]
 
-        def multiply(b, codes, scales, cols, picked, picked_scales, first, start, stop):
+        def multiply(b, codes, scales, cols, picked, part, start, stop):
             nc.tensor.matmul_mx(
                 out=acc[b][:],
                 lhsT=codes[:, cols].bitcast(FP8X4),
                 lhsT_scale=scales[:, cols],
                 rhs=picked[:].bitcast(FP8X4),
-                rhs_scale=picked_scales[first:P, :],
+                rhs_scale=planes[:, part * S : (part + 1) * S],
                 start=start,
                 stop=stop,
             )
 
-        x_picked_scales = gather("x_picked_scales", U8, x_bytes, x_list)
-        h_grouped = interleave("h_grouped", h_raw, J)
-        x_picked = gather("x_picked", U32, x_table, x_list)
+        gather(picked_bytes[:, 0:S], x_bytes, x_list)
+        h_grouped = interleave("h_grouped", h_raw[:], J)
+        gather(picked_bytes[:, S : 2 * S], e_bytes, e_list)
+        gather(picked_bytes[:, 2 * S : 3 * S], f_bytes, f_list)
+        for q in range(4):
+            row = FIRST_ROW + 4 * q
+            nc.sync.dma_start(planes[32 * q : 32 * q + 4, :].bitcast(I32), picked_bytes[row : row + 4, :].bitcast(I32))
+
+        f_table = load_words(stage, "first", f_words)
+
+        gather(x_picked[:], x_table, x_list)
         h_codes, h_scales = quantize("h", h_grouped, J)
-        e_picked_scales = gather("e_picked_scales", U8, e_bytes, e_list)
         for b in range(BLOCKS):
-            multiply(b, h_codes, h_scales, slice(b * P, (b + 1) * P), x_picked, x_picked_scales, 0, True, False)
-        g_grouped = interleave("g_grouped", g_raw, J)
-        f_picked_scales = gather("f_picked_scales", U8, f_bytes, f_list)
-        e_picked = gather("e_picked", U32, e_table, e_list)
-        g_codes, g_scales = quantize("g", g_grouped, J)
-        for b in range(BLOCKS):
-            multiply(b, g_codes, g_scales, slice(b * P, (b + 1) * P), e_picked, e_picked_scales, 4, False, False)
-        f_picked = gather("f_picked", U32, f_table, f_list)
-        for b in range(BLOCKS):
-            r_grouped = interleave("r_grouped%d" % b, r_raw[b], P)
-            r_codes, r_scales = quantize("r%d" % b, r_grouped, P)
-            multiply(b, r_codes, r_scales, slice(0, P), f_picked, f_picked_scales, 8, False, True)
+            multiply(b, h_codes, h_scales, slice(b * P, (b + 1) * P), x_picked, 0, True, False)
+        g_grouped = interleave("g_grouped", g_raw[:], HALF)
+        g_codes, g_scales = quantize("g", g_grouped, HALF)
+
+        late = [("r", 0), ("r", 1), ("g", 2), ("r", 2), ("g", 3), ("r", 3)]
+        late_raw = stage.tile([P, len(late), PACK, P], F32, name="second", align_bytes=64)
+        for i, (part, b) in enumerate(late):
+            load_queries(late_raw[:, i, :, :], gT if part == "g" else rT, b * P, P)
+
+        gather(e_picked[:], e_table, e_list)
+        for b in range(2):
+            multiply(b, g_codes, g_scales, slice(b * P, (b + 1) * P), e_picked, 1, False, False)
+        gather(f_picked[:], f_table, f_list)
+        for i, (part, b) in enumerate(late):
+            grouped = interleave("late_grouped%d" % i, late_raw[:, i, :, :], P)
+            codes, scales = quantize("late%d" % i, grouped, P)
+            if part == "g":
+                multiply(b, codes, scales, slice(0, P), e_picked, 1, False, False)
+                continue
+            multiply(b, codes, scales, slice(0, P), f_picked, 2, False, True)
             best = keep.tile([P, G], F32, name="best%d" % b)
             nc.vector.tensor_reduce(
                 out=best[:],

@@ -18,7 +18,6 @@ PACK = 4
 BLOCKS = J // P
 SCALE_ROWS = K // 32
 FIRST_ROW = P - SCALE_ROWS
-HALF = J // 2
 
 
 def tile_picked_zpq_max_p_kernel(tc, x_words, x_scales, e_words, e_scales, f_words, f_scales, hT, gT, rT, offs, code2, code3, out):
@@ -50,8 +49,8 @@ def tile_picked_zpq_max_p_kernel(tc, x_words, x_scales, e_words, e_scales, f_wor
         def gather(picked, window, offsets):
             nc.vector.tensor_copy(picked, window[:].indirect(offsets[:]))
 
-        def interleave(name, raw, width):
-            tile = keep.tile([P, width, PACK], BF16, name=name, align_bytes=64)
+        def interleave(pool, name, raw, width):
+            tile = pool.tile([P, width, PACK], BF16, name=name, align_bytes=64)
             nc.scalar.copy(
                 out=tile[:].rearrange("p (c i) j -> p c j i", i=4),
                 in_=raw.rearrange("p j (c i) -> p c j i", i=4),
@@ -73,8 +72,8 @@ def tile_picked_zpq_max_p_kernel(tc, x_words, x_scales, e_words, e_scales, f_wor
         f_bytes = load_scales("f_bytes", f_scales, nc.vector)
         f_list = load_list("f_list", code3)
         x_table = load_words(keep, "x_table", x_words)
-        g_raw = stage.tile([P, PACK, HALF], F32, name="second", align_bytes=64)
-        load_queries(g_raw[:], gT, 0, HALF)
+        g_raw = keep.tile([P, PACK, J], F32, name="g_raw")
+        load_queries(g_raw[:], gT, 0, J)
         e_table = load_words(keep, "e_table", e_words)
 
         picked_bytes = keep.tile([P, 3 * S], U8, name="picked_bytes", align_bytes=64)
@@ -97,7 +96,7 @@ def tile_picked_zpq_max_p_kernel(tc, x_words, x_scales, e_words, e_scales, f_wor
             )
 
         gather(picked_bytes[:, 0:S], x_bytes, x_list)
-        h_grouped = interleave("h_grouped", h_raw[:], J)
+        h_grouped = interleave(stage, "second", h_raw[:], J)
         gather(picked_bytes[:, S : 2 * S], e_bytes, e_list)
         gather(picked_bytes[:, 2 * S : 3 * S], f_bytes, f_list)
         for q in range(4):
@@ -110,25 +109,21 @@ def tile_picked_zpq_max_p_kernel(tc, x_words, x_scales, e_words, e_scales, f_wor
         h_codes, h_scales = quantize("h", h_grouped, J)
         for b in range(BLOCKS):
             multiply(b, h_codes, h_scales, slice(b * P, (b + 1) * P), x_picked, 0, True, False)
-        g_grouped = interleave("g_grouped", g_raw[:], HALF)
-        g_codes, g_scales = quantize("g", g_grouped, HALF)
 
-        late = [("r", 0), ("r", 1), ("g", 2), ("r", 2), ("g", 3), ("r", 3)]
-        late_raw = stage.tile([P, len(late), PACK, P], F32, name="second", align_bytes=64)
-        for i, (part, b) in enumerate(late):
-            load_queries(late_raw[:, i, :, :], gT if part == "g" else rT, b * P, P)
+        r_raw = stage.tile([P, BLOCKS, PACK, P], F32, name="second", align_bytes=64)
+        for b in range(BLOCKS):
+            load_queries(r_raw[:, b, :, :], rT, b * P, P)
 
+        g_grouped = interleave(keep, "g_grouped", g_raw[:], J)
         gather(e_picked[:], e_table, e_list)
-        for b in range(2):
+        g_codes, g_scales = quantize("g", g_grouped, J)
+        for b in range(BLOCKS):
             multiply(b, g_codes, g_scales, slice(b * P, (b + 1) * P), e_picked, 1, False, False)
         gather(f_picked[:], f_table, f_list)
-        for i, (part, b) in enumerate(late):
-            grouped = interleave("late_grouped%d" % i, late_raw[:, i, :, :], P)
-            codes, scales = quantize("late%d" % i, grouped, P)
-            if part == "g":
-                multiply(b, codes, scales, slice(0, P), e_picked, 1, False, False)
-                continue
-            multiply(b, codes, scales, slice(0, P), f_picked, 2, False, True)
+        for b in range(BLOCKS):
+            r_grouped = interleave(keep, "r_grouped%d" % b, r_raw[:, b, :, :], P)
+            r_codes, r_scales = quantize("r%d" % b, r_grouped, P)
+            multiply(b, r_codes, r_scales, slice(0, P), f_picked, 2, False, True)
             best = keep.tile([P, G], F32, name="best%d" % b)
             nc.vector.tensor_reduce(
                 out=best[:],

from contextlib import ExitStack

import concourse.mybir as mybir

K, T, S, J, G = 512, 2048, 512, 512, 128
FLOPS = 2 * 3 * K * J * S

F32 = mybir.dt.float32
BF16 = mybir.dt.bfloat16
I32 = mybir.dt.int32
U32 = mybir.dt.uint32
U16 = mybir.dt.uint16
U8 = mybir.dt.uint8
FP8X4 = mybir.dt.float8_e4m3fn_x4

P = 128
PACK = 4
BLOCKS = J // P
SCALE_ROWS = K // 32
FIRST_ROW = P - SCALE_ROWS


def tile_picked_zpq_max_p_kernel(tc, x_words, x_scales, e_words, e_scales, f_words, f_scales, hT, gT, rT, offs, code2, code3, out):
    nc = tc.nc
    with ExitStack() as ctx:
        keep = ctx.enter_context(tc.tile_pool(name="keep", bufs=1))
        stage = ctx.enter_context(tc.tile_pool(name="stage", bufs=1))
        psum = ctx.enter_context(tc.psum_pool(name="psum", bufs=1))

        def load_list(name, src):
            tile = keep.tile([P, S // 16], U16, name=name)
            nc.sync.dma_start(tile[:], src)
            return tile

        def load_words(pool, name, src):
            tile = pool.tile([P, T], U32, name=name, align_bytes=64)
            nc.sync.dma_start(tile[:].bitcast(I32), src[0].rearrange("p n t -> p (n t)").bitcast(I32))
            return tile

        def load_scales(name, src, engine):
            tile = keep.tile([P, T], U8, name=name, align_bytes=64)
            engine.memset(tile[0:FIRST_ROW, :].bitcast(I32), 0)
            nc.scalar.dma_start(tile[FIRST_ROW:P, :].bitcast(I32), src[0].bitcast(I32))
            return tile

        def load_queries(raw, src, first, width):
            nc.sync.dma_start(raw, src.rearrange("(p j) t -> p j t", j=PACK)[:, :, first : first + width])

        def gather(picked, window, offsets):
            nc.vector.tensor_copy(picked, window[:].indirect(offsets[:]))

        def interleave(pool, name, raw, width):
            tile = pool.tile([P, width, PACK], BF16, name=name, align_bytes=64)
            nc.scalar.copy(
                out=tile[:].rearrange("p (c i) j -> p c j i", i=4),
                in_=raw.rearrange("p j (c i) -> p c j i", i=4),
            )
            return tile

        def quantize(name, grouped, width):
            codes = keep.tile([P, width], U32, name=name + "_codes", align_bytes=64)
            scales = keep.tile([P, width], U8, name=name + "_scales", align_bytes=64)
            nc.vector.quantize_mx(out=codes[:].bitcast(FP8X4), scales=scales[:], in_=grouped[:].rearrange("p w j -> p (w j)"))
            return codes, scales

        x_list = load_list("x_list", offs)
        x_bytes = load_scales("x_bytes", x_scales, nc.vector)
        h_raw = stage.tile([P, PACK, J], F32, name="first", align_bytes=64)
        load_queries(h_raw[:], hT, 0, J)
        e_bytes = load_scales("e_bytes", e_scales, nc.gpsimd)
        e_list = load_list("e_list", code2)
        f_bytes = load_scales("f_bytes", f_scales, nc.vector)
        f_list = load_list("f_list", code3)
        x_table = load_words(keep, "x_table", x_words)
        g_raw = keep.tile([P, PACK, J], F32, name="g_raw")
        load_queries(g_raw[:], gT, 0, J)
        e_table = load_words(keep, "e_table", e_words)

        picked_bytes = keep.tile([P, 3 * S], U8, name="picked_bytes", align_bytes=64)
        planes = keep.tile([P, 3 * S], U8, name="planes", align_bytes=64)
        nc.gpsimd.memset(planes[:].bitcast(I32), 0)
        x_picked = keep.tile([P, S], U32, name="x_picked", align_bytes=64)
        e_picked = keep.tile([P, S], U32, name="e_picked", align_bytes=64)
        f_picked = keep.tile([P, S], U32, name="f_picked", align_bytes=64)
        acc = [psum.tile([P, S], F32, name="acc%d" % b) for b in range(BLOCKS)]

        def multiply(b, codes, scales, cols, picked, part, start, stop):
            nc.tensor.matmul_mx(
                out=acc[b][:],
                lhsT=codes[:, cols].bitcast(FP8X4),
                lhsT_scale=scales[:, cols],
                rhs=picked[:].bitcast(FP8X4),
                rhs_scale=planes[:, part * S : (part + 1) * S],
                start=start,
                stop=stop,
            )

        gather(picked_bytes[:, 0:S], x_bytes, x_list)
        h_grouped = interleave(stage, "second", h_raw[:], J)
        gather(picked_bytes[:, S : 2 * S], e_bytes, e_list)
        gather(picked_bytes[:, 2 * S : 3 * S], f_bytes, f_list)
        for q in range(4):
            row = FIRST_ROW + 4 * q
            nc.sync.dma_start(planes[32 * q : 32 * q + 4, :].bitcast(I32), picked_bytes[row : row + 4, :].bitcast(I32))

        f_table = load_words(stage, "first", f_words)

        gather(x_picked[:], x_table, x_list)
        h_codes, h_scales = quantize("h", h_grouped, J)
        for b in range(BLOCKS):
            multiply(b, h_codes, h_scales, slice(b * P, (b + 1) * P), x_picked, 0, True, False)

        r_raw = stage.tile([P, BLOCKS, PACK, P], F32, name="second", align_bytes=64)
        for b in range(BLOCKS):
            load_queries(r_raw[:, b, :, :], rT, b * P, P)

        g_grouped = interleave(keep, "g_grouped", g_raw[:], J)
        gather(e_picked[:], e_table, e_list)
        g_codes, g_scales = quantize("g", g_grouped, J)
        for b in range(BLOCKS):
            multiply(b, g_codes, g_scales, slice(b * P, (b + 1) * P), e_picked, 1, False, False)
        gather(f_picked[:], f_table, f_list)
        for b in range(BLOCKS):
            r_grouped = interleave(keep, "r_grouped%d" % b, r_raw[:, b, :, :], P)
            r_codes, r_scales = quantize("r%d" % b, r_grouped, P)
            multiply(b, r_codes, r_scales, slice(0, P), f_picked, 2, False, True)
            best = keep.tile([P, G], F32, name="best%d" % b)
            nc.vector.tensor_reduce(
                out=best[:],
                in_=acc[b][:].rearrange("p (v m) -> p v m", m=4),
                axis=mybir.AxisListType.X,
                op=mybir.AluOpType.max,
            )
            nc.sync.dma_start(out[b * P : (b + 1) * P, :], best[:])
